import numpy as np
import ml_dtypes


def mxq(x, axis, fmt="e4m3"):
    dtype, down = {"e4m3": (ml_dtypes.float8_e4m3fn, 7), "e5m2": (ml_dtypes.float8_e5m2, 14)}[fmt]
    v = np.moveaxis(np.asarray(x, np.float32).astype(ml_dtypes.bfloat16).astype(np.float64), axis, -1)
    blocks = v.reshape(v.shape[:-1] + (-1, 32))
    amax = np.abs(blocks).max(-1, keepdims=True)
    byte = np.maximum(np.where(amax > 0, np.frexp(amax)[1] - 1 + 127, 0) - down, 1)
    scale = np.exp2(byte - 127.0)
    codes = (blocks / scale).astype(np.float32).astype(dtype).astype(np.float64)
    return np.moveaxis((codes * scale).reshape(v.shape), -1, axis)


WIDE = False


def mx_kscale(k):
    if not WIDE:
        return np.ones(k)
    levels = np.array([10, -10, 5, -5, 0])
    if k % 512:
        return np.exp2(np.random.permutation(np.resize(levels, k // 32))).repeat(32)
    a = np.empty((k // 512, 16))
    for p in range(k // 512):
        a[p, :8] = np.random.permutation(np.resize(levels, 8))
        for g in range(8):
            far = levels[np.abs(levels - a[p, g]) >= 10]
            a[p, g + 8] = far[np.random.randint(len(far))]
    return np.exp2(a.ravel()).repeat(32)


def f64(x):
    return np.asarray(x).astype(np.float64)


def striped(idx):
    return np.tile(idx.reshape(-1, 16).T, (8, 1)).astype(np.uint16)


def unstriped(offs):
    return offs[:16].T.reshape(-1).astype(np.int64)


def pack_weight(w):
    k, n = w.shape
    w = f64(np.asarray(w, np.float32).astype(ml_dtypes.bfloat16)).reshape(k // 32, 32, n)
    amax = np.abs(w).max(1)
    byte = np.clip(np.where(amax > 0, np.frexp(amax)[1] - 1 + 127 - 7, 1), 1, 254)
    scaled = (w * np.exp2(127.0 - byte)[:, None, :]).reshape(k, n).astype(np.float32)
    words = np.ascontiguousarray(scaled.reshape(k // 512, 128, 4, n).transpose(0, 1, 3, 2)).astype(ml_dtypes.float8_e4m3fn).view(np.uint8)
    return words, np.ascontiguousarray(byte.astype(np.uint8).reshape(k // 512, 16, n))


def unpack_weight(words, scales):
    g, p, n, _ = words.shape
    vals = np.ascontiguousarray(words).view(ml_dtypes.float8_e4m3fn).astype(np.float64) * np.repeat(np.exp2(scales.astype(np.float64) - 127.0), 8, axis=1)[..., None]
    return vals.transpose(0, 1, 3, 2).reshape(g * 512, n)


E2M1 = np.array([0.0, 0.5, 1.0, 1.5, 2.0, 3.0, 4.0, 6.0, -0.0, -0.5, -1.0, -1.5, -2.0, -3.0, -4.0, -6.0])


def pack_fp4(w):
    k, n = w.shape
    w = f64(np.asarray(w, np.float32).astype(ml_dtypes.bfloat16)).reshape(k // 32, 32, n)
    amax = np.abs(w).max(1)
    mant, ex = np.frexp(amax / 6.0)
    byte = np.clip(np.where(amax > 0, np.where(mant > 0.5, ex, ex - 1) + 127, 1), 1, 254)
    scaled = (w * np.exp2(127.0 - byte)[:, None, :]).reshape(k, n).astype(np.float32)
    c = np.ascontiguousarray(scaled.reshape(k // 512, 128, 4, n).transpose(0, 1, 3, 2)).astype(ml_dtypes.float4_e2m1fn).view(np.uint8) & 0xF
    words = (c[..., 0::2] | (c[..., 1::2] << 4)).reshape(k // 512, 128, 2 * n)
    return np.ascontiguousarray(words), np.ascontiguousarray(byte.astype(np.uint8).reshape(k // 512, 16, n))


def unpack_fp4(words, scales):
    g, _, n = scales.shape
    words = np.ascontiguousarray(words).reshape(g, 128, n, 2)
    nib = np.empty((g, 128, n, 4), np.uint8)
    nib[..., 0::2] = words & 0xF
    nib[..., 1::2] = words >> 4
    vals = E2M1[nib] * np.repeat(np.exp2(scales.astype(np.float64) - 127.0), 8, axis=1)[..., None]
    return vals.transpose(0, 1, 3, 2).reshape(g * 512, n)


K, T, S, N, H = 512, 1024, 512, 256, 512


def setup_inputs():
    n = np.random.standard_normal
    s = mx_kscale(K)[:, None]
    u = mx_kscale(H)
    packed_xT = pack_weight(n((K, T)) * s)
    packed_w1 = pack_fp4(n((K, H)) / np.sqrt(K) / s)
    packed_w2 = pack_fp4(n((K, H)) / np.sqrt(K) / s)
    packed_w3 = pack_fp4(n((H, N)) / np.sqrt(H) / u[:, None])
    return {
        "x_words": packed_xT[0],
        "x_scales": packed_xT[1],
        "w1_words": packed_w1[0],
        "w1_scales": packed_w1[1],
        "w2_words": packed_w2[0],
        "w2_scales": packed_w2[1],
        "sig": (np.random.uniform(0.3, 1.2, (H, S))).astype(np.float32),
        "cap": (np.random.uniform(0.5, 1.2, (H, S))).astype(np.float32),
        "unit": (np.random.uniform(0.6, 1.4, (H, 1)) * u[:, None]).astype(np.float32),
        "w3_words": packed_w3[0],
        "w3_scales": packed_w3[1],
        "offs": striped(np.random.permutation(T)[:S]),
        "reg": striped(np.random.permutation(S)),
    }


def reference(x_words, x_scales, w1_words, w1_scales, w2_words, w2_scales, sig, cap, unit, w3_words, w3_scales, offs, reg):
    xq = unpack_weight(x_words, x_scales)[:, unstriped(offs)]
    sr = unpack_fp4(w1_words, w1_scales).T @ xq
    sf = unpack_fp4(w2_words, w2_scales).T @ xq
    drc = (sr - sf) / f64(sig)
    ad = np.abs(drc)
    nrm = ad.mean(axis=1, keepdims=True)
    gd = drc / (nrm + 0.2)
    hid = f64(unit) * (np.minimum(np.maximum(gd, -1.0 * f64(cap)), f64(cap)) + gd[:, unstriped(reg)])
    return unpack_fp4(w3_words, w3_scales).T @ mxq(hid, 0, "e4m3")

@@ -1,0 +1,175 @@
+from contextlib import ExitStack
+
+import concourse.mybir as mybir
+from concourse.masks import make_identity
+
+K, T, S, N, H = 512, 1024, 512, 256, 512
+FLOPS = 2 * (2 * K * H * S + H * N * S)
+
+F32 = mybir.dt.float32
+BF16 = mybir.dt.bfloat16
+I32 = mybir.dt.int32
+U32 = mybir.dt.uint32
+U16 = mybir.dt.uint16
+U8 = mybir.dt.uint8
+FP8X4 = mybir.dt.float8_e4m3fn_x4
+FP4X4 = mybir.dt.float4_e2m1fn_x4
+ALU = mybir.AluOpType
+ACT = mybir.ActivationFunctionType
+
+P = 128
+PACK = 4
+HALF = S // 2
+LIST_ROWS = 16
+SIGN_UNIT = 2.0 ** -60
+SPARE = 8
+SCALAR_GATHER_SLOTS = (2, 3)
+
+
+def load_scale_rows(queue, plane, scales):
+    for q in range(4):
+        rows = scales[0, 4 * q : 4 * q + 4, :].bitcast(I32).rearrange("r n -> (r n)")
+        queue.dma_start(out=plane[32 * q : 32 * q + 32, :].bitcast(I32), in_=rows.partition_broadcast(8))
+
+
+def tile_picked_ydmddi_clip_p_kernel(
+    tc, x_words, x_scales, w1_words, w1_scales, w2_words, w2_scales, sig, cap, unit, w3_words, w3_scales, offs, reg, out
+):
+    nc = tc.nc
+    with ExitStack() as ctx:
+        keep = ctx.enter_context(tc.tile_pool(name="keep", bufs=1))
+        psum = ctx.enter_context(tc.psum_pool(name="psum", bufs=1))
+
+        def sb(name, cols, dtype):
+            return keep.tile([P, cols], dtype, name=name, align_bytes=64)
+
+        offs_sb = keep.tile([P, S // LIST_ROWS], U16, name="offs_sb")
+        reg_sb = keep.tile([P, S // LIST_ROWS], U16, name="reg_sb")
+        xw = sb("xw", T, U32)
+        xs = sb("xs", T, U8)
+        w1w, w2w, w3w = sb("w1w", 2 * H, U8), sb("w2w", 2 * H, U8), sb("w3w", 2 * N, U8)
+        w1s, w2s, w3s = sb("w1s", H, U8), sb("w2s", H, U8), sb("w3s", N, U8)
+        sig_sb = [sb(f"sig{t}", S, F32) for t in range(PACK)]
+        cap_sb = [sb(f"cap{t}", S, F32) for t in range(PACK)]
+        unit_sb = sb("unit_sb", PACK, F32)
+        sig_rows = sig.rearrange("(p t) j -> p t j", t=PACK)
+        cap_rows = cap.rearrange("(p t) j -> p t j", t=PACK)
+
+        load_scale_rows(nc.sync, xs, x_scales)
+        nc.sync.dma_start(offs_sb[:], offs)
+        nc.sync.dma_start(out=sig_sb[0][:], in_=sig_rows[:, 0, :])
+        nc.sync.dma_start(out=xw[:].bitcast(I32), in_=x_words[0].rearrange("p n t -> p (n t)").bitcast(I32))
+        nc.sync.dma_start(out=w1w[:].bitcast(I32), in_=w1_words[0].bitcast(I32))
+        load_scale_rows(nc.gpsimd, w2s, w2_scales)
+        load_scale_rows(nc.scalar, w1s, w1_scales)
+        nc.sync.dma_start(out=w2w[:].bitcast(I32), in_=w2_words[0].bitcast(I32))
+        for t in range(1, PACK):
+            nc.sync.dma_start(out=sig_sb[t][:], in_=sig_rows[:, t, :])
+        for t in range(PACK):
+            nc.sync.dma_start(out=cap_sb[t][:], in_=cap_rows[:, t, :])
+        nc.sync.dma_start(reg_sb[:], reg)
+        nc.sync.dma_start(out=unit_sb[:], in_=unit.rearrange("(p t) o -> p (t o)", t=PACK))
+        nc.sync.dma_start(out=w3w[:].bitcast(I32), in_=w3_words[0].bitcast(I32))
+        load_scale_rows(nc.sync, w3s, w3_scales)
+
+        ident = sb("ident", P, F32)
+        make_identity(nc, ident[:])
+
+        squares = [sb(f"sq{t}", S, F32) for t in range(PACK)]
+        nc.vector.tensor_tensor(out=squares[0][:], in0=sig_sb[0][:], in1=sig_sb[0][:], op=ALU.mult)
+        diff_banks = [psum.tile([P, S], F32, name=f"diff_bank{t}") for t in range(PACK)]
+        picked_w, picked_s = [], []
+        for b in range(S // P):
+            lst = offs_sb[:, b * P // LIST_ROWS : (b + 1) * P // LIST_ROWS]
+            gw, gs = sb(f"gw{b}", P, U32), sb(f"gs{b}", P, U8)
+            nc.vector.tensor_copy(out=gw[:], in_=xw[:].indirect(lst))
+            nc.vector.tensor_copy(out=gs[:], in_=xs[:].indirect(lst))
+            picked_w.append(gw)
+            picked_s.append(gs)
+        diff_t = []
+        for b in range(S // P):
+            sr = psum.tile([P, H], F32, name=f"sr{b}", tag=f"bank{2 * (b % 2)}")
+            sf = psum.tile([P, H], F32, name=f"sf{b}", tag=f"bank{2 * (b % 2) + 1}")
+            for acc, ww, ws in ((sr, w1w, w1s), (sf, w2w, w2s)):
+                nc.tensor.matmul_mx(out=acc[:], lhsT=picked_w[b][:].bitcast(FP8X4), lhsT_scale=picked_s[b][:],
+                                    rhs=ww[:].bitcast(FP4X4), rhs_scale=ws[:], start=True, stop=True)
+            sr_sb = sb(f"sr_sb{b}", H, F32)
+            nc.scalar.copy(out=sr_sb[:].rearrange("p (t m) -> p t m", t=PACK), in_=sr[:].rearrange("p (m t) -> p t m", t=PACK))
+            d = sb(f"diff_t{b}", H, F32)
+            nc.vector.tensor_tensor(out=d[:].rearrange("p (t m) -> p t m", t=PACK), in0=sr_sb[:].rearrange("p (t m) -> p t m", t=PACK),
+                                    in1=sf[:].rearrange("p (m t) -> p t m", t=PACK), op=ALU.subtract)
+            diff_t.append(d)
+        for b in range(S // P):
+            for t in range(PACK):
+                nc.tensor.transpose(diff_banks[t][:, b * P : (b + 1) * P], diff_t[b][:, t * P : (t + 1) * P], ident[:])
+
+        inv_sig = []
+        for t in range(PACK):
+            sgn = sb(f"sgn{t}", S, F32)
+            nc.gpsimd.tensor_scalar(out=sgn[:], in0=sig_sb[t][:], scalar1=SIGN_UNIT, scalar2=-SIGN_UNIT, op0=ALU.min, op1=ALU.max)
+            sq = squares[t]
+            if t == 1:
+                nc.vector.tensor_tensor(out=sq[:], in0=sig_sb[t][:], in1=sig_sb[t][:], op=ALU.mult)
+            elif t > 1:
+                nc.scalar.activation(out=sq[:], in_=sig_sb[t][:], func=ACT.Square)
+            mag = sb(f"mag{t}", S, F32)
+            nc.scalar.activation(out=mag[:], in_=sq[:], func=ACT.Abs_reciprocal_sqrt)
+            inv = sb(f"inv{t}", S, F32)
+            nc.gpsimd.tensor_tensor(out=inv[:], in0=mag[:], in1=sgn[:], op=ALU.mult)
+            inv_sig.append(inv)
+
+        ones = sb("ones", SPARE, F32)
+        nc.gpsimd.memset(ones[:], 1.0)
+        neg = [sb(f"neg{t}", S + SPARE, F32) for t in range(PACK)]
+        for t in range(PACK):
+            nc.gpsimd.tensor_scalar(out=neg[t][:, S:], in0=ones[:], scalar1=0.2 * S / SPARE, scalar2=0.0, op0=ALU.mult, op1=ALU.add)
+
+        planes = keep.tile([P, 2, PACK, HALF], BF16, name="planes", align_bytes=64)
+        mags = sb("mags", S + SPARE, BF16)
+        for t in range(PACK):
+            nc.vector.scalar_tensor_tensor(out=neg[t][:, :S], in0=diff_banks[t][:], scalar=-1.0 / SIGN_UNIT, in1=inv_sig[t][:], op0=ALU.mult, op1=ALU.mult)
+            den = sb(f"den{t}", 1, F32)
+            nc.scalar.activation(out=mags[:], in_=neg[t][:], func=ACT.Abs, scale=1.0 / S, accum_out=den[:])
+            nden = sb(f"nden{t}", 1, F32)
+            nc.scalar.activation(out=nden[:], in_=den[:], func=ACT.Copy, scale=-1.0)
+            low = sb(f"low{t}", S, F32)
+            nc.vector.scalar_tensor_tensor(out=low[:], in0=cap_sb[t][:], scalar=den[:], in1=neg[t][:, :S], op0=ALU.mult, op1=ALU.min)
+            rden = sb(f"rden{t}", 1, F32)
+            nc.vector.reciprocal(out=rden[:], in_=nden[:])
+            gain = sb(f"gain{t}", 1, F32)
+            nc.scalar.activation(out=gain[:], in_=rden[:], func=ACT.Copy, scale=unit_sb[:, t : t + 1])
+            pieces = 2 if t == PACK - 1 else 1
+            width = S // pieces
+            for h in range(pieces):
+                cols = slice(h * width, (h + 1) * width)
+                lst = reg_sb[:, h * width // LIST_ROWS : (h + 1) * width // LIST_ROWS]
+                clip = sb(f"clip{t}_{h}", width, F32)
+                nc.vector.scalar_tensor_tensor(out=clip[:], in0=cap_sb[t][:, cols], scalar=nden[:], in1=low[:, cols], op0=ALU.mult, op1=ALU.max)
+                total = sb(f"total{t}_{h}", width, F32)
+                if t in SCALAR_GATHER_SLOTS:
+                    fetched = sb(f"fetched{t}_{h}", width, F32)
+                    nc.scalar.activation(out=fetched[:], in_=neg[t][:].indirect(lst), func=ACT.Copy)
+                    nc.vector.tensor_tensor(out=total[:], in0=fetched[:], in1=clip[:], op=ALU.add)
+                else:
+                    nc.vector.tensor_tensor(out=total[:], in0=neg[t][:].indirect(lst), in1=clip[:], op=ALU.add)
+                if pieces == 1:
+                    nc.scalar.activation(out=planes[:, :, t, :], in_=total[:].rearrange("p (h c) -> p h c", h=2), func=ACT.Copy, scale=gain[:])
+                else:
+                    nc.scalar.activation(out=planes[:, h, t, :], in_=total[:], func=ACT.Copy, scale=gain[:])
+
+        for h in range(2):
+            woven = sb(f"woven{h}", PACK * HALF, BF16)
+            nc.vector.tensor_copy(out=woven[:].rearrange("p (c i t) -> p c t i", i=4, t=PACK),
+                                  in_=planes[:, h, :, :].rearrange("p t (c i) -> p c t i", i=4))
+            codes, code_scales = sb(f"codes{h}", HALF, U32), sb(f"code_scales{h}", HALF, U8)
+            nc.vector.quantize_mx(out=codes[:].bitcast(FP8X4), scales=code_scales[:], in_=woven[:])
+            for u in range(N // P):
+                acc = psum.tile([P, HALF], F32, name=f"out{h}_{u}", tag=f"bank{2 * h + u}")
+                nc.tensor.matmul_mx(out=acc[:], lhsT=w3w[:, 2 * P * u : 2 * P * (u + 1)].bitcast(FP4X4), lhsT_scale=w3s[:, P * u : P * (u + 1)],
+                                    rhs=codes[:].bitcast(FP8X4), rhs_scale=code_scales[:], start=True, stop=True)
+                res = sb(f"res{h}_{u}", HALF, F32)
+                if u == 0:
+                    nc.scalar.copy(out=res[:], in_=acc[:])
+                else:
+                    nc.vector.tensor_copy(out=res[:], in_=acc[:])
+                nc.sync.dma_start(out=out[u * P : (u + 1) * P, h * HALF : (h + 1) * HALF], in_=res[:])

@@ -21,13 +21,14 @@ P = 128
 PACK = 4
 HALF = S // 2
 LIST_ROWS = 16
-SIGN_UNIT = 2.0 ** -60
 SPARE = 8
-SCALAR_GATHER_SLOTS = (2, 3)
+SCALAR_GATHER_SLOTS = (0, 1, 2, 3)
+VECTOR_SIGN_SLOTS = (0, 1)
+PICK = 256
 
 
-def load_scale_rows(queue, plane, scales):
-    for q in range(4):
+def load_scale_rows(queue, plane, scales, quadrants=range(4)):
+    for q in quadrants:
         rows = scales[0, 4 * q : 4 * q + 4, :].bitcast(I32).rearrange("r n -> (r n)")
         queue.dma_start(out=plane[32 * q : 32 * q + 32, :].bitcast(I32), in_=rows.partition_broadcast(8))
 
@@ -49,25 +50,36 @@ def tile_picked_ydmddi_clip_p_kernel(
         xs = sb("xs", T, U8)
         w1w, w2w, w3w = sb("w1w", 2 * H, U8), sb("w2w", 2 * H, U8), sb("w3w", 2 * N, U8)
         w1s, w2s, w3s = sb("w1s", H, U8), sb("w2s", H, U8), sb("w3s", N, U8)
-        sig_sb = [sb(f"sig{t}", S, F32) for t in range(PACK)]
-        cap_sb = [sb(f"cap{t}", S, F32) for t in range(PACK)]
+        sig01 = sb("sig01", 2 * S, F32)
+        sig23 = [sb(f"sig{t}", S, F32) for t in (2, 3)]
+        sig_sb = [sig01[:, :S], sig01[:, S:], sig23[0][:], sig23[1][:]]
+        cap_pairs = [sb(f"cap{g}", 2 * S, F32) for g in range(2)]
+        cap_sb = [cap_pairs[t // 2][:, (t % 2) * S : (t % 2 + 1) * S] for t in range(PACK)]
         unit_sb = sb("unit_sb", PACK, F32)
-        sig_rows = sig.rearrange("(p t) j -> p t j", t=PACK)
-        cap_rows = cap.rearrange("(p t) j -> p t j", t=PACK)
+        sig_rows = sig.rearrange("(p t) j -> p (t j)", t=PACK)
+        cap_rows = cap.rearrange("(p t) j -> p (t j)", t=PACK)
+
+        ones = sb("ones", SPARE, F32)
+        nc.vector.memset(ones[:], 1.0)
+        warm = sb("warm", SPARE, F32)
+        nc.scalar.activation(out=warm[:], in_=ones[:], func=ACT.Abs_reciprocal_sqrt)
+        neg = [sb(f"neg{t}", S + SPARE, F32) for t in range(PACK)]
+        for t in range(PACK):
+            nc.vector.tensor_scalar(out=neg[t][:, S:], in0=ones[:], scalar1=0.2 * S / SPARE, scalar2=None, op0=ALU.mult)
 
         load_scale_rows(nc.sync, xs, x_scales)
         nc.sync.dma_start(offs_sb[:], offs)
-        nc.sync.dma_start(out=sig_sb[0][:], in_=sig_rows[:, 0, :])
+        nc.sync.dma_start(out=sig01[:], in_=sig_rows[:, : 2 * S])
         nc.sync.dma_start(out=xw[:].bitcast(I32), in_=x_words[0].rearrange("p n t -> p (n t)").bitcast(I32))
         nc.sync.dma_start(out=w1w[:].bitcast(I32), in_=w1_words[0].bitcast(I32))
-        load_scale_rows(nc.gpsimd, w2s, w2_scales)
-        load_scale_rows(nc.scalar, w1s, w1_scales)
+        load_scale_rows(nc.sync, w1s, w1_scales)
         nc.sync.dma_start(out=w2w[:].bitcast(I32), in_=w2_words[0].bitcast(I32))
-        for t in range(1, PACK):
-            nc.sync.dma_start(out=sig_sb[t][:], in_=sig_rows[:, t, :])
-        for t in range(PACK):
-            nc.sync.dma_start(out=cap_sb[t][:], in_=cap_rows[:, t, :])
+        load_scale_rows(nc.sync, w2s, w2_scales)
+        for t in (2, 3):
+            nc.sync.dma_start(out=sig_sb[t], in_=sig_rows[:, t * S : (t + 1) * S])
         nc.sync.dma_start(reg_sb[:], reg)
+        for g in range(2):
+            nc.sync.dma_start(out=cap_pairs[g][:], in_=cap_rows[:, 2 * g * S : 2 * (g + 1) * S])
         nc.sync.dma_start(out=unit_sb[:], in_=unit.rearrange("(p t) o -> p (t o)", t=PACK))
         nc.sync.dma_start(out=w3w[:].bitcast(I32), in_=w3_words[0].bitcast(I32))
         load_scale_rows(nc.sync, w3s, w3_scales)
@@ -75,23 +87,38 @@ def tile_picked_ydmddi_clip_p_kernel(
         ident = sb("ident", P, F32)
         make_identity(nc, ident[:])
 
-        squares = [sb(f"sq{t}", S, F32) for t in range(PACK)]
-        nc.vector.tensor_tensor(out=squares[0][:], in0=sig_sb[0][:], in1=sig_sb[0][:], op=ALU.mult)
-        diff_banks = [psum.tile([P, S], F32, name=f"diff_bank{t}") for t in range(PACK)]
+        signs, mags_inv, inv_sig = {}, {}, {}
+
+        def prepare(t):
+            sq = sb(f"sq{t}", S, F32)
+            nc.scalar.activation(out=sq[:], in_=sig_sb[t], func=ACT.Square)
+            mags_inv[t] = sb(f"mag{t}", S, F32)
+            nc.scalar.activation(out=mags_inv[t][:], in_=sq[:], func=ACT.Abs_reciprocal_sqrt)
+            signs[t] = sb(f"sgn{t}", S, F32)
+            if t in VECTOR_SIGN_SLOTS:
+                nc.vector.tensor_scalar(out=signs[t][:], in0=sig_sb[t], scalar1=0.0, scalar2=0.5, op0=ALU.is_ge, op1=ALU.subtract)
+            else:
+                nc.scalar.activation(out=signs[t][:], in_=sig_sb[t], func=ACT.Sign)
+
+        def invert(t):
+            inv_sig[t] = sb(f"inv{t}", S, F32)
+            nc.vector.tensor_tensor(out=inv_sig[t][:], in0=mags_inv[t][:], in1=signs[t][:], op=ALU.mult)
+
         picked_w, picked_s = [], []
-        for b in range(S // P):
-            lst = offs_sb[:, b * P // LIST_ROWS : (b + 1) * P // LIST_ROWS]
-            gw, gs = sb(f"gw{b}", P, U32), sb(f"gs{b}", P, U8)
+        for c in range(S // PICK):
+            lst = offs_sb[:, c * PICK // LIST_ROWS : (c + 1) * PICK // LIST_ROWS]
+            gw, gs = sb(f"gw{c}", PICK, U32), sb(f"gs{c}", PICK, U8)
             nc.vector.tensor_copy(out=gw[:], in_=xw[:].indirect(lst))
             nc.vector.tensor_copy(out=gs[:], in_=xs[:].indirect(lst))
-            picked_w.append(gw)
-            picked_s.append(gs)
+            for b in range(PICK // P):
+                picked_w.append(gw[:, b * P : (b + 1) * P])
+                picked_s.append(gs[:, b * P : (b + 1) * P])
         diff_t = []
         for b in range(S // P):
-            sr = psum.tile([P, H], F32, name=f"sr{b}", tag=f"bank{2 * (b % 2)}")
-            sf = psum.tile([P, H], F32, name=f"sf{b}", tag=f"bank{2 * (b % 2) + 1}")
+            sr = psum.tile([P, H], F32, name=f"sr{b}", tag=f"bank{b}")
+            sf = psum.tile([P, H], F32, name=f"sf{b}", tag=f"bank{4 + b}")
             for acc, ww, ws in ((sr, w1w, w1s), (sf, w2w, w2s)):
-                nc.tensor.matmul_mx(out=acc[:], lhsT=picked_w[b][:].bitcast(FP8X4), lhsT_scale=picked_s[b][:],
+                nc.tensor.matmul_mx(out=acc[:], lhsT=picked_w[b].bitcast(FP8X4), lhsT_scale=picked_s[b],
                                     rhs=ww[:].bitcast(FP4X4), rhs_scale=ws[:], start=True, stop=True)
             sr_sb = sb(f"sr_sb{b}", H, F32)
             nc.scalar.copy(out=sr_sb[:].rearrange("p (t m) -> p t m", t=PACK), in_=sr[:].rearrange("p (m t) -> p t m", t=PACK))
@@ -99,41 +126,28 @@ def tile_picked_ydmddi_clip_p_kernel(
             nc.vector.tensor_tensor(out=d[:].rearrange("p (t m) -> p t m", t=PACK), in0=sr_sb[:].rearrange("p (t m) -> p t m", t=PACK),
                                     in1=sf[:].rearrange("p (m t) -> p t m", t=PACK), op=ALU.subtract)
             diff_t.append(d)
-        for b in range(S // P):
-            for t in range(PACK):
+        diff_banks = [psum.tile([P, S], F32, name=f"diff_bank{t}", tag=f"bank{t}") for t in range(PACK)]
+        for t in range(PACK):
+            for b in range(S // P):
                 nc.tensor.transpose(diff_banks[t][:, b * P : (b + 1) * P], diff_t[b][:, t * P : (t + 1) * P], ident[:])
-
-        inv_sig = []
-        for t in range(PACK):
-            sgn = sb(f"sgn{t}", S, F32)
-            nc.gpsimd.tensor_scalar(out=sgn[:], in0=sig_sb[t][:], scalar1=SIGN_UNIT, scalar2=-SIGN_UNIT, op0=ALU.min, op1=ALU.max)
-            sq = squares[t]
-            if t == 1:
-                nc.vector.tensor_tensor(out=sq[:], in0=sig_sb[t][:], in1=sig_sb[t][:], op=ALU.mult)
-            elif t > 1:
-                nc.scalar.activation(out=sq[:], in_=sig_sb[t][:], func=ACT.Square)
-            mag = sb(f"mag{t}", S, F32)
-            nc.scalar.activation(out=mag[:], in_=sq[:], func=ACT.Abs_reciprocal_sqrt)
-            inv = sb(f"inv{t}", S, F32)
-            nc.gpsimd.tensor_tensor(out=inv[:], in0=mag[:], in1=sgn[:], op=ALU.mult)
-            inv_sig.append(inv)
-
-        ones = sb("ones", SPARE, F32)
-        nc.gpsimd.memset(ones[:], 1.0)
-        neg = [sb(f"neg{t}", S + SPARE, F32) for t in range(PACK)]
-        for t in range(PACK):
-            nc.gpsimd.tensor_scalar(out=neg[t][:, S:], in0=ones[:], scalar1=0.2 * S / SPARE, scalar2=0.0, op0=ALU.mult, op1=ALU.add)
 
         planes = keep.tile([P, 2, PACK, HALF], BF16, name="planes", align_bytes=64)
         mags = sb("mags", S + SPARE, BF16)
-        for t in range(PACK):
-            nc.vector.scalar_tensor_tensor(out=neg[t][:, :S], in0=diff_banks[t][:], scalar=-1.0 / SIGN_UNIT, in1=inv_sig[t][:], op0=ALU.mult, op1=ALU.mult)
+        dens = {}
+
+        def normalise(t):
+            factor = -2.0 if t in VECTOR_SIGN_SLOTS else -1.0
+            nc.vector.scalar_tensor_tensor(out=neg[t][:, :S], in0=diff_banks[t][:], scalar=factor, in1=inv_sig[t][:], op0=ALU.mult, op1=ALU.mult)
             den = sb(f"den{t}", 1, F32)
             nc.scalar.activation(out=mags[:], in_=neg[t][:], func=ACT.Abs, scale=1.0 / S, accum_out=den[:])
             nden = sb(f"nden{t}", 1, F32)
             nc.scalar.activation(out=nden[:], in_=den[:], func=ACT.Copy, scale=-1.0)
+            dens[t] = (den, nden)
+
+        def combine(t):
+            den, nden = dens[t]
             low = sb(f"low{t}", S, F32)
-            nc.vector.scalar_tensor_tensor(out=low[:], in0=cap_sb[t][:], scalar=den[:], in1=neg[t][:, :S], op0=ALU.mult, op1=ALU.min)
+            nc.vector.scalar_tensor_tensor(out=low[:], in0=cap_sb[t], scalar=den[:], in1=neg[t][:, :S], op0=ALU.mult, op1=ALU.min)
             rden = sb(f"rden{t}", 1, F32)
             nc.vector.reciprocal(out=rden[:], in_=nden[:])
             gain = sb(f"gain{t}", 1, F32)
@@ -156,6 +170,16 @@ def tile_picked_ydmddi_clip_p_kernel(
                     nc.scalar.activation(out=planes[:, :, t, :], in_=total[:].rearrange("p (h c) -> p h c", h=2), func=ACT.Copy, scale=gain[:])
                 else:
                     nc.scalar.activation(out=planes[:, h, t, :], in_=total[:], func=ACT.Copy, scale=gain[:])
+
+        prepare(0)
+        invert(0)
+        normalise(0)
+        for t in range(PACK):
+            if t + 1 < PACK:
+                prepare(t + 1)
+                invert(t + 1)
+                normalise(t + 1)
+            combine(t)
 
         for h in range(2):
             woven = sb(f"woven{h}", PACK * HALF, BF16)

@@ -21,9 +21,10 @@ P = 128
 PACK = 4
 HALF = S // 2
 LIST_ROWS = 16
+SIGN_UNIT = 2.0 ** -60
 SPARE = 8
-SCALAR_GATHER_SLOTS = (0, 1, 2, 3)
-VECTOR_SIGN_SLOTS = (0, 1)
+SCALAR_GATHER_SLOTS = ()
+VECTOR_SIGN_SLOTS = ()
 PICK = 256
 
 
@@ -51,8 +52,8 @@ def tile_picked_ydmddi_clip_p_kernel(
         w1w, w2w, w3w = sb("w1w", 2 * H, U8), sb("w2w", 2 * H, U8), sb("w3w", 2 * N, U8)
         w1s, w2s, w3s = sb("w1s", H, U8), sb("w2s", H, U8), sb("w3s", N, U8)
         sig01 = sb("sig01", 2 * S, F32)
-        sig23 = [sb(f"sig{t}", S, F32) for t in (2, 3)]
-        sig_sb = [sig01[:, :S], sig01[:, S:], sig23[0][:], sig23[1][:]]
+        sig23 = sb("sig23", 2 * S, F32)
+        sig_sb = [sig01[:, :S], sig01[:, S:], sig23[:, :S], sig23[:, S:]]
         cap_pairs = [sb(f"cap{g}", 2 * S, F32) for g in range(2)]
         cap_sb = [cap_pairs[t // 2][:, (t % 2) * S : (t % 2 + 1) * S] for t in range(PACK)]
         unit_sb = sb("unit_sb", PACK, F32)
@@ -69,14 +70,13 @@ def tile_picked_ydmddi_clip_p_kernel(
 
         load_scale_rows(nc.sync, xs, x_scales)
         nc.sync.dma_start(offs_sb[:], offs)
-        nc.sync.dma_start(out=sig01[:], in_=sig_rows[:, : 2 * S])
         nc.sync.dma_start(out=xw[:].bitcast(I32), in_=x_words[0].rearrange("p n t -> p (n t)").bitcast(I32))
         nc.sync.dma_start(out=w1w[:].bitcast(I32), in_=w1_words[0].bitcast(I32))
+        nc.sync.dma_start(out=sig01[:], in_=sig_rows[:, : 2 * S])
         load_scale_rows(nc.sync, w1s, w1_scales)
         nc.sync.dma_start(out=w2w[:].bitcast(I32), in_=w2_words[0].bitcast(I32))
         load_scale_rows(nc.sync, w2s, w2_scales)
-        for t in (2, 3):
-            nc.sync.dma_start(out=sig_sb[t], in_=sig_rows[:, t * S : (t + 1) * S])
+        nc.sync.dma_start(out=sig23[:], in_=sig_rows[:, 2 * S :])
         nc.sync.dma_start(reg_sb[:], reg)
         for g in range(2):
             nc.sync.dma_start(out=cap_pairs[g][:], in_=cap_rows[:, 2 * g * S : 2 * (g + 1) * S])
@@ -89,20 +89,22 @@ def tile_picked_ydmddi_clip_p_kernel(
 
         signs, mags_inv, inv_sig = {}, {}, {}
 
-        def prepare(t):
+        def magnitude(t, square_on_vector):
             sq = sb(f"sq{t}", S, F32)
-            nc.scalar.activation(out=sq[:], in_=sig_sb[t], func=ACT.Square)
+            if square_on_vector:
+                nc.vector.tensor_tensor(out=sq[:], in0=sig_sb[t], in1=sig_sb[t], op=ALU.mult)
+            else:
+                nc.scalar.activation(out=sq[:], in_=sig_sb[t], func=ACT.Square)
             mags_inv[t] = sb(f"mag{t}", S, F32)
             nc.scalar.activation(out=mags_inv[t][:], in_=sq[:], func=ACT.Abs_reciprocal_sqrt)
-            signs[t] = sb(f"sgn{t}", S, F32)
-            if t in VECTOR_SIGN_SLOTS:
-                nc.vector.tensor_scalar(out=signs[t][:], in0=sig_sb[t], scalar1=0.0, scalar2=0.5, op0=ALU.is_ge, op1=ALU.subtract)
-            else:
-                nc.scalar.activation(out=signs[t][:], in_=sig_sb[t], func=ACT.Sign)
 
-        def invert(t):
+        def sign(engine, g, src):
+            signs[g] = sb(f"sgn{g}", 2 * S, F32)
+            engine.tensor_scalar(out=signs[g][:], in0=src[:], scalar1=SIGN_UNIT, scalar2=-SIGN_UNIT, op0=ALU.min, op1=ALU.max)
+
+        def invert(engine, t):
             inv_sig[t] = sb(f"inv{t}", S, F32)
-            nc.vector.tensor_tensor(out=inv_sig[t][:], in0=mags_inv[t][:], in1=signs[t][:], op=ALU.mult)
+            engine.tensor_tensor(out=inv_sig[t][:], in0=mags_inv[t][:], in1=signs[t // 2][:, (t % 2) * S : (t % 2 + 1) * S], op=ALU.mult)
 
         picked_w, picked_s = [], []
         for c in range(S // PICK):
@@ -133,66 +135,114 @@ def tile_picked_ydmddi_clip_p_kernel(
 
         planes = keep.tile([P, 2, PACK, HALF], BF16, name="planes", align_bytes=64)
         mags = sb("mags", S + SPARE, BF16)
-        dens = {}
+        dens = [sb(f"dens{g}", 2, F32) for g in range(2)]
+        ndens = [sb(f"ndens{g}", 2, F32) for g in range(2)]
+        gains = [sb(f"gains{g}", 2, F32) for g in range(2)]
+        lows = [sb(f"low{t}", S, F32) for t in range(PACK)]
+        clips = [sb(f"clips{g}", 2 * S, F32) for g in range(2)]
+        fetched = [sb(f"fetched{g}", 2 * S, F32) for g in range(2)]
+        totals = [sb(f"totals{g}", 2 * S, F32) for g in range(2)]
 
-        def normalise(t):
-            factor = -2.0 if t in VECTOR_SIGN_SLOTS else -1.0
-            nc.vector.scalar_tensor_tensor(out=neg[t][:, :S], in0=diff_banks[t][:], scalar=factor, in1=inv_sig[t][:], op0=ALU.mult, op1=ALU.mult)
-            den = sb(f"den{t}", 1, F32)
-            nc.scalar.activation(out=mags[:], in_=neg[t][:], func=ACT.Abs, scale=1.0 / S, accum_out=den[:])
-            nden = sb(f"nden{t}", 1, F32)
-            nc.scalar.activation(out=nden[:], in_=den[:], func=ACT.Copy, scale=-1.0)
-            dens[t] = (den, nden)
+        def column(tiles, t):
+            return tiles[t // 2][:, t % 2 : t % 2 + 1]
 
-        def combine(t):
-            den, nden = dens[t]
-            low = sb(f"low{t}", S, F32)
-            nc.vector.scalar_tensor_tensor(out=low[:], in0=cap_sb[t], scalar=den[:], in1=neg[t][:, :S], op0=ALU.mult, op1=ALU.min)
-            rden = sb(f"rden{t}", 1, F32)
-            nc.vector.reciprocal(out=rden[:], in_=nden[:])
-            gain = sb(f"gain{t}", 1, F32)
-            nc.scalar.activation(out=gain[:], in_=rden[:], func=ACT.Copy, scale=unit_sb[:, t : t + 1])
-            pieces = 2 if t == PACK - 1 else 1
-            width = S // pieces
-            for h in range(pieces):
-                cols = slice(h * width, (h + 1) * width)
-                lst = reg_sb[:, h * width // LIST_ROWS : (h + 1) * width // LIST_ROWS]
-                clip = sb(f"clip{t}_{h}", width, F32)
-                nc.vector.scalar_tensor_tensor(out=clip[:], in0=cap_sb[t][:, cols], scalar=nden[:], in1=low[:, cols], op0=ALU.mult, op1=ALU.max)
-                total = sb(f"total{t}_{h}", width, F32)
-                if t in SCALAR_GATHER_SLOTS:
-                    fetched = sb(f"fetched{t}_{h}", width, F32)
-                    nc.scalar.activation(out=fetched[:], in_=neg[t][:].indirect(lst), func=ACT.Copy)
-                    nc.vector.tensor_tensor(out=total[:], in0=fetched[:], in1=clip[:], op=ALU.add)
-                else:
-                    nc.vector.tensor_tensor(out=total[:], in0=neg[t][:].indirect(lst), in1=clip[:], op=ALU.add)
-                if pieces == 1:
-                    nc.scalar.activation(out=planes[:, :, t, :], in_=total[:].rearrange("p (h c) -> p h c", h=2), func=ACT.Copy, scale=gain[:])
-                else:
-                    nc.scalar.activation(out=planes[:, h, t, :], in_=total[:], func=ACT.Copy, scale=gain[:])
+        def by_half(tile, t):
+            return tile[:].rearrange("p (h s c) -> p h s c", h=2, s=2)[:, :, t % 2, :]
 
-        prepare(0)
-        invert(0)
-        normalise(0)
-        for t in range(PACK):
-            if t + 1 < PACK:
-                prepare(t + 1)
-                invert(t + 1)
-                normalise(t + 1)
-            combine(t)
+        def halves(ap):
+            return ap.rearrange("p (h c) -> p h c", h=2)
 
+        def scale(t):
+            nc.vector.scalar_tensor_tensor(out=neg[t][:, :S], in0=diff_banks[t][:], scalar=-1.0 / SIGN_UNIT, in1=inv_sig[t][:], op0=ALU.mult, op1=ALU.mult)
+
+        def measure(t):
+            nc.scalar.activation(out=mags[:], in_=neg[t][:], func=ACT.Abs, scale=1.0 / S, accum_out=column(dens, t))
+
+        def negate(g):
+            nc.scalar.activation(out=ndens[g][:], in_=dens[g][:], func=ACT.Copy, scale=-1.0)
+
+        def lower(t):
+            nc.vector.scalar_tensor_tensor(out=lows[t][:], in0=cap_sb[t], scalar=column(dens, t), in1=neg[t][:, :S], op0=ALU.mult, op1=ALU.min)
+
+        def upper(t):
+            nc.vector.scalar_tensor_tensor(out=by_half(clips[t // 2], t), in0=halves(cap_sb[t]), scalar=column(ndens, t), in1=halves(lows[t][:]), op0=ALU.mult, op1=ALU.max)
+
+        def reciprocal(g):
+            rden = sb(f"rden{g}", 2, F32)
+            nc.vector.reciprocal(out=rden[:], in_=ndens[g][:])
+            return rden
+
+        def gain(g, rden):
+            nc.vector.tensor_tensor(out=gains[g][:], in0=rden[:], in1=unit_sb[:, 2 * g : 2 * g + 2], op=ALU.mult)
+
+        def fetch(t, h):
+            lst = reg_sb[:, h * HALF // LIST_ROWS : (h + 1) * HALF // LIST_ROWS]
+            nc.scalar.activation(out=by_half(fetched[t // 2], t)[:, h, :], in_=neg[t][:].indirect(lst), func=ACT.Copy)
+
+        def add(g, cols):
+            nc.vector.tensor_tensor(out=totals[g][:, cols], in0=fetched[g][:, cols], in1=clips[g][:, cols], op=ALU.add)
+
+        def round_out(t, hs):
+            nc.scalar.activation(out=planes[:, hs, t, :], in_=by_half(totals[t // 2], t)[:, hs, :], func=ACT.Copy, scale=column(gains, t))
+
+        magnitude(0, False)
+        magnitude(1, True)
+        sign(nc.vector, 0, sig01)
+        invert(nc.vector, 0)
+        invert(nc.gpsimd, 1)
+        sign(nc.gpsimd, 1, sig23)
+        scale(0)
+        measure(0)
+        scale(1)
+        measure(1)
+        negate(0)
+        for t in (2, 3):
+            magnitude(t, False)
+            invert(nc.gpsimd, t)
+        scale(2)
+        lower(0)
+        lower(1)
+        scale(3)
+        upper(0)
+        upper(1)
+        rden = reciprocal(0)
+        for t in (0, 1):
+            for h in range(2):
+                fetch(t, h)
+        measure(2)
+        measure(3)
+        negate(1)
+        add(0, slice(0, 2 * S))
+        gain(0, rden)
+        lower(2)
+        lower(3)
+        rden = reciprocal(1)
+        upper(2)
+        upper(3)
+        gain(1, rden)
         for h in range(2):
-            woven = sb(f"woven{h}", PACK * HALF, BF16)
-            nc.vector.tensor_copy(out=woven[:].rearrange("p (c i t) -> p c t i", i=4, t=PACK),
+            for t in (2, 3):
+                fetch(t, h)
+        round_out(0, slice(0, 2))
+        round_out(1, slice(0, 2))
+        for h in range(2):
+            add(1, slice(h * S, (h + 1) * S))
+            for t in (2, 3):
+                round_out(t, slice(h, h + 1))
+
+        woven = [sb(f"woven{h}", PACK * HALF, BF16) for h in range(2)]
+        for h in range(2):
+            nc.vector.tensor_copy(out=woven[h][:].rearrange("p (c i t) -> p c t i", i=4, t=PACK),
                                   in_=planes[:, h, :, :].rearrange("p t (c i) -> p c t i", i=4))
+        for h in range(2):
             codes, code_scales = sb(f"codes{h}", HALF, U32), sb(f"code_scales{h}", HALF, U8)
-            nc.vector.quantize_mx(out=codes[:].bitcast(FP8X4), scales=code_scales[:], in_=woven[:])
+            nc.vector.quantize_mx(out=codes[:].bitcast(FP8X4), scales=code_scales[:], in_=woven[h][:])
             for u in range(N // P):
                 acc = psum.tile([P, HALF], F32, name=f"out{h}_{u}", tag=f"bank{2 * h + u}")
                 nc.tensor.matmul_mx(out=acc[:], lhsT=w3w[:, 2 * P * u : 2 * P * (u + 1)].bitcast(FP4X4), lhsT_scale=w3s[:, P * u : P * (u + 1)],
                                     rhs=codes[:].bitcast(FP8X4), rhs_scale=code_scales[:], start=True, stop=True)
                 res = sb(f"res{h}_{u}", HALF, F32)
-                if u == 0:
+                if (h, u) != (1, 1):
                     nc.scalar.copy(out=res[:], in_=acc[:])
                 else:
                     nc.vector.tensor_copy(out=res[:], in_=acc[:])

from contextlib import ExitStack

import concourse.mybir as mybir
from concourse.masks import make_identity

K, T, S, N, H = 512, 1024, 512, 256, 512
FLOPS = 2 * (2 * K * H * S + H * N * S)

F32 = mybir.dt.float32
BF16 = mybir.dt.bfloat16
I32 = mybir.dt.int32
U32 = mybir.dt.uint32
U16 = mybir.dt.uint16
U8 = mybir.dt.uint8
FP8X4 = mybir.dt.float8_e4m3fn_x4
FP4X4 = mybir.dt.float4_e2m1fn_x4
ALU = mybir.AluOpType
ACT = mybir.ActivationFunctionType

P = 128
PACK = 4
HALF = S // 2
LIST_ROWS = 16
SIGN_UNIT = 2.0 ** -60
SPARE = 8
SCALAR_GATHER_SLOTS = ()
VECTOR_SIGN_SLOTS = ()
PICK = 256


def load_scale_rows(queue, plane, scales, quadrants=range(4)):
    for q in quadrants:
        rows = scales[0, 4 * q : 4 * q + 4, :].bitcast(I32).rearrange("r n -> (r n)")
        queue.dma_start(out=plane[32 * q : 32 * q + 32, :].bitcast(I32), in_=rows.partition_broadcast(8))


def tile_picked_ydmddi_clip_p_kernel(
    tc, x_words, x_scales, w1_words, w1_scales, w2_words, w2_scales, sig, cap, unit, w3_words, w3_scales, offs, reg, out
):
    nc = tc.nc
    with ExitStack() as ctx:
        keep = ctx.enter_context(tc.tile_pool(name="keep", bufs=1))
        psum = ctx.enter_context(tc.psum_pool(name="psum", bufs=1))

        def sb(name, cols, dtype):
            return keep.tile([P, cols], dtype, name=name, align_bytes=64)

        offs_sb = keep.tile([P, S // LIST_ROWS], U16, name="offs_sb")
        reg_sb = keep.tile([P, S // LIST_ROWS], U16, name="reg_sb")
        xw = sb("xw", T, U32)
        xs = sb("xs", T, U8)
        w1w, w2w, w3w = sb("w1w", 2 * H, U8), sb("w2w", 2 * H, U8), sb("w3w", 2 * N, U8)
        w1s, w2s, w3s = sb("w1s", H, U8), sb("w2s", H, U8), sb("w3s", N, U8)
        sig01 = sb("sig01", 2 * S, F32)
        sig23 = sb("sig23", 2 * S, F32)
        sig_sb = [sig01[:, :S], sig01[:, S:], sig23[:, :S], sig23[:, S:]]
        cap_pairs = [sb(f"cap{g}", 2 * S, F32) for g in range(2)]
        cap_sb = [cap_pairs[t // 2][:, (t % 2) * S : (t % 2 + 1) * S] for t in range(PACK)]
        unit_sb = sb("unit_sb", PACK, F32)
        sig_rows = sig.rearrange("(p t) j -> p (t j)", t=PACK)
        cap_rows = cap.rearrange("(p t) j -> p (t j)", t=PACK)

        ones = sb("ones", SPARE, F32)
        nc.vector.memset(ones[:], 1.0)
        warm = sb("warm", SPARE, F32)
        nc.scalar.activation(out=warm[:], in_=ones[:], func=ACT.Abs_reciprocal_sqrt)
        neg = [sb(f"neg{t}", S + SPARE, F32) for t in range(PACK)]
        for t in range(PACK):
            nc.vector.tensor_scalar(out=neg[t][:, S:], in0=ones[:], scalar1=0.2 * S / SPARE, scalar2=None, op0=ALU.mult)

        load_scale_rows(nc.sync, xs, x_scales)
        nc.sync.dma_start(offs_sb[:], offs)
        nc.sync.dma_start(out=xw[:].bitcast(I32), in_=x_words[0].rearrange("p n t -> p (n t)").bitcast(I32))
        nc.sync.dma_start(out=w1w[:].bitcast(I32), in_=w1_words[0].bitcast(I32))
        nc.sync.dma_start(out=sig01[:], in_=sig_rows[:, : 2 * S])
        load_scale_rows(nc.sync, w1s, w1_scales)
        nc.sync.dma_start(out=w2w[:].bitcast(I32), in_=w2_words[0].bitcast(I32))
        load_scale_rows(nc.sync, w2s, w2_scales)
        nc.sync.dma_start(out=sig23[:], in_=sig_rows[:, 2 * S :])
        nc.sync.dma_start(reg_sb[:], reg)
        for g in range(2):
            nc.sync.dma_start(out=cap_pairs[g][:], in_=cap_rows[:, 2 * g * S : 2 * (g + 1) * S])
        nc.sync.dma_start(out=unit_sb[:], in_=unit.rearrange("(p t) o -> p (t o)", t=PACK))
        nc.sync.dma_start(out=w3w[:].bitcast(I32), in_=w3_words[0].bitcast(I32))
        load_scale_rows(nc.sync, w3s, w3_scales)

        ident = sb("ident", P, F32)
        make_identity(nc, ident[:])

        signs, mags_inv, inv_sig = {}, {}, {}

        def magnitude(t, square_on_vector):
            sq = sb(f"sq{t}", S, F32)
            if square_on_vector:
                nc.vector.tensor_tensor(out=sq[:], in0=sig_sb[t], in1=sig_sb[t], op=ALU.mult)
            else:
                nc.scalar.activation(out=sq[:], in_=sig_sb[t], func=ACT.Square)
            mags_inv[t] = sb(f"mag{t}", S, F32)
            nc.scalar.activation(out=mags_inv[t][:], in_=sq[:], func=ACT.Abs_reciprocal_sqrt)

        def sign(engine, g, src):
            signs[g] = sb(f"sgn{g}", 2 * S, F32)
            engine.tensor_scalar(out=signs[g][:], in0=src[:], scalar1=SIGN_UNIT, scalar2=-SIGN_UNIT, op0=ALU.min, op1=ALU.max)

        def invert(engine, t):
            inv_sig[t] = sb(f"inv{t}", S, F32)
            engine.tensor_tensor(out=inv_sig[t][:], in0=mags_inv[t][:], in1=signs[t // 2][:, (t % 2) * S : (t % 2 + 1) * S], op=ALU.mult)

        picked_w, picked_s = [], []
        for c in range(S // PICK):
            lst = offs_sb[:, c * PICK // LIST_ROWS : (c + 1) * PICK // LIST_ROWS]
            gw, gs = sb(f"gw{c}", PICK, U32), sb(f"gs{c}", PICK, U8)
            nc.vector.tensor_copy(out=gw[:], in_=xw[:].indirect(lst))
            nc.vector.tensor_copy(out=gs[:], in_=xs[:].indirect(lst))
            for b in range(PICK // P):
                picked_w.append(gw[:, b * P : (b + 1) * P])
                picked_s.append(gs[:, b * P : (b + 1) * P])
        diff_t = []
        for b in range(S // P):
            sr = psum.tile([P, H], F32, name=f"sr{b}", tag=f"bank{b}")
            sf = psum.tile([P, H], F32, name=f"sf{b}", tag=f"bank{4 + b}")
            for acc, ww, ws in ((sr, w1w, w1s), (sf, w2w, w2s)):
                nc.tensor.matmul_mx(out=acc[:], lhsT=picked_w[b].bitcast(FP8X4), lhsT_scale=picked_s[b],
                                    rhs=ww[:].bitcast(FP4X4), rhs_scale=ws[:], start=True, stop=True)
            sr_sb = sb(f"sr_sb{b}", H, F32)
            nc.scalar.copy(out=sr_sb[:].rearrange("p (t m) -> p t m", t=PACK), in_=sr[:].rearrange("p (m t) -> p t m", t=PACK))
            d = sb(f"diff_t{b}", H, F32)
            nc.vector.tensor_tensor(out=d[:].rearrange("p (t m) -> p t m", t=PACK), in0=sr_sb[:].rearrange("p (t m) -> p t m", t=PACK),
                                    in1=sf[:].rearrange("p (m t) -> p t m", t=PACK), op=ALU.subtract)
            diff_t.append(d)
        diff_banks = [psum.tile([P, S], F32, name=f"diff_bank{t}", tag=f"bank{t}") for t in range(PACK)]
        for t in range(PACK):
            for b in range(S // P):
                nc.tensor.transpose(diff_banks[t][:, b * P : (b + 1) * P], diff_t[b][:, t * P : (t + 1) * P], ident[:])

        planes = keep.tile([P, 2, PACK, HALF], BF16, name="planes", align_bytes=64)
        mags = sb("mags", S + SPARE, BF16)
        dens = [sb(f"dens{g}", 2, F32) for g in range(2)]
        ndens = [sb(f"ndens{g}", 2, F32) for g in range(2)]
        gains = [sb(f"gains{g}", 2, F32) for g in range(2)]
        lows = [sb(f"low{t}", S, F32) for t in range(PACK)]
        clips = [sb(f"clips{g}", 2 * S, F32) for g in range(2)]
        fetched = [sb(f"fetched{g}", 2 * S, F32) for g in range(2)]
        totals = [sb(f"totals{g}", 2 * S, F32) for g in range(2)]

        def column(tiles, t):
            return tiles[t // 2][:, t % 2 : t % 2 + 1]

        def by_half(tile, t):
            return tile[:].rearrange("p (h s c) -> p h s c", h=2, s=2)[:, :, t % 2, :]

        def halves(ap):
            return ap.rearrange("p (h c) -> p h c", h=2)

        def scale(t):
            nc.vector.scalar_tensor_tensor(out=neg[t][:, :S], in0=diff_banks[t][:], scalar=-1.0 / SIGN_UNIT, in1=inv_sig[t][:], op0=ALU.mult, op1=ALU.mult)

        def measure(t):
            nc.scalar.activation(out=mags[:], in_=neg[t][:], func=ACT.Abs, scale=1.0 / S, accum_out=column(dens, t))

        def negate(g):
            nc.scalar.activation(out=ndens[g][:], in_=dens[g][:], func=ACT.Copy, scale=-1.0)

        def lower(t):
            nc.vector.scalar_tensor_tensor(out=lows[t][:], in0=cap_sb[t], scalar=column(dens, t), in1=neg[t][:, :S], op0=ALU.mult, op1=ALU.min)

        def upper(t):
            nc.vector.scalar_tensor_tensor(out=by_half(clips[t // 2], t), in0=halves(cap_sb[t]), scalar=column(ndens, t), in1=halves(lows[t][:]), op0=ALU.mult, op1=ALU.max)

        def reciprocal(g):
            rden = sb(f"rden{g}", 2, F32)
            nc.vector.reciprocal(out=rden[:], in_=ndens[g][:])
            return rden

        def gain(g, rden):
            nc.vector.tensor_tensor(out=gains[g][:], in0=rden[:], in1=unit_sb[:, 2 * g : 2 * g + 2], op=ALU.mult)

        def fetch(t, h):
            lst = reg_sb[:, h * HALF // LIST_ROWS : (h + 1) * HALF // LIST_ROWS]
            nc.scalar.activation(out=by_half(fetched[t // 2], t)[:, h, :], in_=neg[t][:].indirect(lst), func=ACT.Copy)

        def add(g, cols):
            nc.vector.tensor_tensor(out=totals[g][:, cols], in0=fetched[g][:, cols], in1=clips[g][:, cols], op=ALU.add)

        def round_out(t, hs):
            nc.scalar.activation(out=planes[:, hs, t, :], in_=by_half(totals[t // 2], t)[:, hs, :], func=ACT.Copy, scale=column(gains, t))

        magnitude(0, False)
        magnitude(1, True)
        sign(nc.vector, 0, sig01)
        invert(nc.vector, 0)
        invert(nc.gpsimd, 1)
        sign(nc.gpsimd, 1, sig23)
        scale(0)
        measure(0)
        scale(1)
        measure(1)
        negate(0)
        for t in (2, 3):
            magnitude(t, False)
            invert(nc.gpsimd, t)
        scale(2)
        lower(0)
        lower(1)
        scale(3)
        upper(0)
        upper(1)
        rden = reciprocal(0)
        for t in (0, 1):
            for h in range(2):
                fetch(t, h)
        measure(2)
        measure(3)
        negate(1)
        add(0, slice(0, 2 * S))
        gain(0, rden)
        lower(2)
        lower(3)
        rden = reciprocal(1)
        upper(2)
        upper(3)
        gain(1, rden)
        for h in range(2):
            for t in (2, 3):
                fetch(t, h)
        round_out(0, slice(0, 2))
        round_out(1, slice(0, 2))
        for h in range(2):
            add(1, slice(h * S, (h + 1) * S))
            for t in (2, 3):
                round_out(t, slice(h, h + 1))

        woven = [sb(f"woven{h}", PACK * HALF, BF16) for h in range(2)]
        for h in range(2):
            nc.vector.tensor_copy(out=woven[h][:].rearrange("p (c i t) -> p c t i", i=4, t=PACK),
                                  in_=planes[:, h, :, :].rearrange("p t (c i) -> p c t i", i=4))
        for h in range(2):
            codes, code_scales = sb(f"codes{h}", HALF, U32), sb(f"code_scales{h}", HALF, U8)
            nc.vector.quantize_mx(out=codes[:].bitcast(FP8X4), scales=code_scales[:], in_=woven[h][:])
            for u in range(N // P):
                acc = psum.tile([P, HALF], F32, name=f"out{h}_{u}", tag=f"bank{2 * h + u}")
                nc.tensor.matmul_mx(out=acc[:], lhsT=w3w[:, 2 * P * u : 2 * P * (u + 1)].bitcast(FP4X4), lhsT_scale=w3s[:, P * u : P * (u + 1)],
                                    rhs=codes[:].bitcast(FP8X4), rhs_scale=code_scales[:], start=True, stop=True)
                res = sb(f"res{h}_{u}", HALF, F32)
                if (h, u) != (1, 1):
                    nc.scalar.copy(out=res[:], in_=acc[:])
                else:
                    nc.vector.tensor_copy(out=res[:], in_=acc[:])
                nc.sync.dma_start(out=out[u * P : (u + 1) * P, h * HALF : (h + 1) * HALF], in_=res[:])
